import numpy as np
import ml_dtypes


def mxq(x, axis, fmt="e4m3"):
    dtype, down = {"e4m3": (ml_dtypes.float8_e4m3fn, 7), "e5m2": (ml_dtypes.float8_e5m2, 14)}[fmt]
    v = np.moveaxis(np.asarray(x, np.float32).astype(ml_dtypes.bfloat16).astype(np.float64), axis, -1)
    blocks = v.reshape(v.shape[:-1] + (-1, 32))
    amax = np.abs(blocks).max(-1, keepdims=True)
    byte = np.maximum(np.where(amax > 0, np.frexp(amax)[1] - 1 + 127, 0) - down, 1)
    scale = np.exp2(byte - 127.0)
    codes = (blocks / scale).astype(np.float32).astype(dtype).astype(np.float64)
    return np.moveaxis((codes * scale).reshape(v.shape), -1, axis)


WIDE = False


def mx_kscale(k):
    if not WIDE:
        return np.ones(k)
    levels = np.array([10, -10, 5, -5, 0])
    if k % 512:
        return np.exp2(np.random.permutation(np.resize(levels, k // 32))).repeat(32)
    a = np.empty((k // 512, 16))
    for p in range(k // 512):
        a[p, :8] = np.random.permutation(np.resize(levels, 8))
        for g in range(8):
            far = levels[np.abs(levels - a[p, g]) >= 10]
            a[p, g + 8] = far[np.random.randint(len(far))]
    return np.exp2(a.ravel()).repeat(32)


def f64(x):
    return np.asarray(x).astype(np.float64)


def striped(idx):
    return np.tile(np.asarray(idx).reshape(-1, 16).T, (8, 1)).astype(np.uint16)


def unstriped(offs):
    return offs[:16].T.reshape(-1).astype(np.int64)


E2M1 = np.array([0.0, 0.5, 1.0, 1.5, 2.0, 3.0, 4.0, 6.0, -0.0, -0.5, -1.0, -1.5, -2.0, -3.0, -4.0, -6.0])


def pack_weight(w, fmt):
    k, n = w.shape
    w = f64(np.asarray(w, np.float32).astype(ml_dtypes.bfloat16)).reshape(k // 32, 32, n)
    amax = np.abs(w).max(1)
    if fmt == "e4m3":
        byte = np.frexp(amax)[1] - 1 + 127 - 7
    else:
        mant, ex = np.frexp(amax / 6.0)
        byte = np.where(mant > 0.5, ex, ex - 1) + 127
    byte = np.clip(np.where(amax > 0, byte, 1), 1, 254)
    scaled = (w * np.exp2(127.0 - byte)[:, None, :]).reshape(k, n).astype(np.float32)
    by_word = np.ascontiguousarray(scaled.reshape(k // 512, 128, 4, n).transpose(0, 1, 3, 2))
    if fmt == "e4m3":
        words = by_word.astype(ml_dtypes.float8_e4m3fn).view(np.uint8)
    else:
        c = by_word.astype(ml_dtypes.float4_e2m1fn).view(np.uint8) & 0xF
        words = (c[..., 0::2] | (c[..., 1::2] << 4)).reshape(k // 512, 128, 2 * n)
    return np.ascontiguousarray(words), np.ascontiguousarray(byte.astype(np.uint8).reshape(k // 512, 16, n))


def unpack_weight(words, scales, fmt):
    g, _, n = scales.shape
    words = np.ascontiguousarray(words).reshape(g, 128, n, -1)
    if fmt == "e4m3":
        vals = words.view(ml_dtypes.float8_e4m3fn).astype(np.float64)
    else:
        nib = np.empty((g, 128, n, 4), np.uint8)
        nib[..., 0::2] = words & 0xF
        nib[..., 1::2] = words >> 4
        vals = E2M1[nib]
    vals = vals * np.repeat(np.exp2(scales.astype(np.float64) - 127.0), 8, axis=1)[..., None]
    return vals.transpose(0, 1, 3, 2).reshape(g * 512, n)


def bf(x):
    return np.asarray(x, np.float32).astype(ml_dtypes.bfloat16)


def planes(Y):
    r, m = Y.shape
    b = f64(bf(Y)).reshape(r // 32, 32, m)
    amax = np.abs(b).max(1)
    byte = np.clip(np.where(amax > 0, np.frexp(amax)[1] - 1 + 127 - 7, 1), 1, 254)
    codes = (b * np.exp2(127.0 - byte)[:, None, :]).reshape(r, m).astype(np.float32).astype(ml_dtypes.float8_e4m3fn).view(np.uint8)
    words = codes.reshape(r // 512, 128, 4, m).transpose(0, 1, 3, 2)
    return np.ascontiguousarray(words), np.ascontiguousarray(byte.astype(np.uint8).reshape(r // 512, 16, m))


D, T, I, Q, E, Z, M = 512, 2048, 512, 256, 512, 1024, 1024


def setup_inputs():
    n = np.random.standard_normal
    idx = np.random.permutation(T)[:I]
    idx2 = np.random.permutation(Z)[:I]
    idx3 = np.random.permutation(M)[:Q]
    fd = mx_kscale(D)
    fi = mx_kscale(I)
    ti = np.ones(T)
    ti[idx] = fi
    keysp = pack_weight(n((D, T)) / fd[:, None], "e2m1")
    return {
        "query": (n((D, Q)) * 1.0 / np.sqrt(D) * fd[:, None]).astype(np.float32),
        "query2": (n((D, Q)) * 1.0 / np.sqrt(D) * fd[:, None]).astype(np.float32),
        "keys_words": keysp[0],
        "keys_scales": keysp[1],
        "pages": (n((D, Z)) / fd[:, None]).astype(np.float32),
        "os": (np.random.uniform(0.02, 0.08, (1, I)) * fi).astype(np.float32),
        "vals": (n((E, T)) / ti).astype(np.float32),
        "member": (n((E, M))).astype(np.float32),
        "offs": striped(idx),
        "offs2": striped(idx2),
        "offs3": striped(idx3),
    }


def reference(query, query2, keys_words, keys_scales, pages, os, vals, member, offs, offs2, offs3):
    idx = unstriped(offs)
    idx2 = unstriped(offs2)
    idx3 = unstriped(offs3)
    keysu = unpack_weight(keys_words, keys_scales, "e2m1")
    queryq = mxq(f64(query), 0, "e4m3")
    a = queryq.T @ keysu
    query2q = mxq(f64(query2), 0, "e4m3")
    pagesq = mxq(f64(pages), 0, "e4m3")
    h0 = query2q.T @ pagesq
    s = np.maximum(a[:, idx], h0[:, idx2])
    w = np.maximum(s, 0.0)
    wo1 = w * f64(os)
    wt1 = wo1.T
    vt1 = f64(vals)[:, idx].T
    vt1q = mxq(vt1, 0, "e4m3")
    wt1q = mxq(wt1, 0, "e4m3")
    o = vt1q.T @ wt1q
    y = np.abs(o - f64(member)[:, idx3])
    words, scales = planes(y)
    return y, words, scales

@@ -1,0 +1,321 @@
+from contextlib import ExitStack
+
+import concourse.mybir as mybir
+from concourse.masks import make_identity
+
+D, T, I, Q, E, Z, M = 512, 2048, 512, 256, 512, 1024, 1024
+FLOPS = 2 * Q * D * T + 2 * Q * D * Z + 2 * E * I * Q
+
+F32 = mybir.dt.float32
+BF16 = mybir.dt.bfloat16
+I32 = mybir.dt.int32
+U32 = mybir.dt.uint32
+U16 = mybir.dt.uint16
+U8 = mybir.dt.uint8
+FP8X4 = mybir.dt.float8_e4m3fn_x4
+FP4X4 = mybir.dt.float4_e2m1fn_x4
+ALU = mybir.AluOpType
+ACT = mybir.ActivationFunctionType
+
+P = 128
+PACK = 4
+BANK = 512
+Q_TILES = Q // P
+
+
+def tile_attend_crosslarger_distanceout_lean_pl_kernel(
+    tc, query, query2, keys_words, keys_scales, pages, slot_factor, vals, member, offs, offs2, offs3, out_0, out_1, out_2
+):
+    nc = tc.nc
+    with ExitStack() as ctx:
+        lists = ctx.enter_context(tc.tile_pool(name="lists", bufs=1))
+        sb = ctx.enter_context(tc.tile_pool(name="sb", bufs=1))
+        psum = ctx.enter_context(tc.psum_pool(name="psum", bufs=1))
+
+        over = {"a_picked1": "pages_grouped1", "h_picked0": "vals0", "v_grouped0": "vals1", "v_grouped1": "vals2", "v1_codes": "vals3", "v_grouped2": "member0", "v_grouped3": "member1", "y0": "m_picked1_0", "v3_codes": "member2", "y2": "member3"}
+
+        def sbuf(name, shape, dtype):
+            return sb.tile(shape, dtype, name=name, tag=over.get(name, name), align_bytes=64)
+
+        def clock(name, ap):
+            c = sbuf(name, [P, 1], F32)
+            nc.gpsimd.tensor_copy(out=c[:], in_=ap)
+
+        def wide_bank(shape):
+            return psum.tile(shape, F32, name="wide_bank", bufs=6)
+
+        def vector_copy(out, in_):
+            nc.vector.tensor_copy(out=out, in_=in_)
+
+        def scalar_copy(out, in_):
+            nc.scalar.activation(out=out, in_=in_, func=ACT.Copy)
+
+        def by_lines(grouped, planes):
+            return (
+                grouped.rearrange("p (c i) t -> p c t i", i=4),
+                planes.rearrange("p t (c i) -> p c t i", i=4),
+            )
+
+        def mx_tiles(name, width):
+            return sbuf(name + "_codes", [P, width], U32), sbuf(name + "_scales", [P, width], U8)
+
+        def quantize(operand, grouped, cols=slice(None)):
+            codes, scales = operand
+            nc.vector.quantize_mx(
+                out=codes[:, cols].bitcast(FP8X4), scales=scales[:, cols], in_=grouped[:].rearrange("p c t -> p (c t)")
+            )
+
+        def product(bank, stationary, cols, moving_codes, moving_scales):
+            codes, scales = stationary
+            nc.tensor.matmul_mx(
+                out=bank[:],
+                lhsT=codes[:, cols].bitcast(FP8X4),
+                lhsT_scale=scales[:, cols],
+                rhs=moving_codes,
+                rhs_scale=moving_scales,
+                start=True,
+                stop=True,
+            )
+
+        def block(n, width):
+            return slice(n * width, (n + 1) * width)
+
+        key_scales = sbuf("key_scales", [P, T], U8)
+        nc.vector.memset(key_scales[:].bitcast(I32), 0)
+        ident = sbuf("ident", [P, P], F32)
+        make_identity(nc, ident[:])
+
+        q_raw = sbuf("q_raw", [P, PACK, Q], F32)
+        nc.sync.dma_start(out=q_raw[:], in_=query.rearrange("(p t) q -> p t q", t=PACK))
+        key_words = sbuf("key_words", [P, 2 * T], U8)
+        nc.sync.dma_start(out=key_words[:].bitcast(I32), in_=keys_words[0].bitcast(I32))
+        for quad in range(4):
+            nc.sync.dma_start(
+                out=key_scales[32 * quad : 32 * quad + 4, :].bitcast(I32),
+                in_=keys_scales[0, 4 * quad : 4 * quad + 4, :].bitcast(I32),
+            )
+        token_list = lists.tile([P, I // 16], U16, name="token_list")
+        nc.sync.dma_start(token_list[:], offs)
+        q2_raw = sbuf("q2_raw", [P, PACK, Q], F32)
+        nc.sync.dma_start(out=q2_raw[:], in_=query2.rearrange("(p t) q -> p t q", t=PACK))
+        pages_rows = pages.rearrange("(p t) z -> p t z", t=PACK)
+        pages_raw = [sbuf("pages_raw%d" % c, [P, PACK, BANK], F32) for c in range(Z // BANK)]
+        for c in range(Z // BANK):
+            nc.sync.dma_start(out=pages_raw[c][:], in_=pages_rows[:, :, block(c, BANK)])
+        page_list = lists.tile([P, I // 16], U16, name="page_list")
+        nc.sync.dma_start(page_list[:], offs2)
+        member_list = lists.tile([P, Q // 16], U16, name="member_list")
+        nc.sync.dma_start(member_list[:], offs3)
+        factor = sbuf("factor", [P, PACK], F32)
+        nc.sync.dma_start(out=factor[:], in_=slot_factor.rearrange("o (p t) -> (o p) t", t=PACK))
+        vals_rows = vals.rearrange("(p r) t -> r p t", r=PACK)
+        vals_sb = [sbuf("vals%d" % r, [P, T], F32) for r in range(PACK)]
+        for r in range(PACK):
+            nc.sync.dma_start(out=vals_sb[r][:], in_=vals_rows[r])
+        member_rows = member.rearrange("(p r) m -> r p m", r=PACK)
+        member_sb = [sbuf("member%d" % r, [P, M], F32) for r in range(PACK)]
+        for r in range(PACK):
+            nc.sync.dma_start(out=member_sb[r][:], in_=member_rows[r])
+
+        q_grouped = sbuf("q_grouped", [P, Q, PACK], BF16)
+        q2_grouped = sbuf("q2_grouped", [P, Q, PACK], BF16)
+        pages_grouped = [sbuf("pages_grouped%d" % c, [P, BANK, PACK], BF16) for c in range(Z // BANK)]
+        q_mx, q2_mx, w_mx, y_mx = (mx_tiles(name, Q) for name in ("q", "q2", "w", "y"))
+        pages_mx = [mx_tiles("pages%d" % c, BANK) for c in range(Z // BANK)]
+        v_mx = {}
+        a_sb = [sbuf("a%d" % j, [P, T], F32) for j in range(Q_TILES)]
+        h_sb = [sbuf("h%d" % j, [P, Z], F32) for j in range(Q_TILES)]
+        a_picked = {}
+        h_picked = {}
+        w_dealt = [sbuf("w_dealt%d" % j, [P, PACK, P], F32) for j in range(Q_TILES)]
+        w_grouped = sbuf("w_grouped", [P, Q, PACK], BF16)
+        v_picked = [sbuf("v_picked%d" % r, [P, I], BF16) for r in range(PACK)]
+        v_grouped = {}
+        m_picked = {}
+        diff = sbuf("diff", [P, Q_TILES, PACK, P], F32)
+        y_grouped = [sbuf("y_grouped%d" % j, [P, P, PACK], BF16) for j in range(Q_TILES)]
+        y_rows = out_0.rearrange("(p r) q -> r p q", r=PACK)
+        banks = {}
+
+        def score_keys(j, c):
+            bank = wide_bank([P, BANK])
+            product(
+                bank, q_mx, block(j, P), key_words[:, block(c, 2 * BANK)].bitcast(FP4X4), key_scales[:, block(c, BANK)]
+            )
+            banks.setdefault(("a", j, c), bank)
+
+        def empty_keys(j, c, copy):
+            copy(a_sb[j][:, block(c, BANK)], banks[("a", j, c)][:])
+
+        def score_pages(j, c):
+            bank = wide_bank([P, BANK])
+            codes, scales = pages_mx[c]
+            product(bank, q2_mx, block(j, P), codes[:].bitcast(FP8X4), scales[:])
+            banks.setdefault(("h", j, c), bank)
+
+        def empty_pages(j, c, copy):
+            copy(h_sb[j][:, block(c, BANK)], banks[("h", j, c)][:])
+
+        def pick_keys(j, copy):
+            a_picked.setdefault(j, sbuf("a_picked%d" % j, [P, I], F32))
+            copy(a_picked[j][:], a_sb[j][:].indirect(token_list[:]))
+
+        def pick_pages(j, copy):
+            h_picked.setdefault(j, sbuf("h_picked%d" % j, [P, I], F32))
+            copy(h_picked[j][:], h_sb[j][:].indirect(page_list[:]))
+
+        def pick_values(r, copy):
+            copy(v_picked[r][:], vals_sb[r][:].indirect(token_list[:]))
+
+        def pick_members(r, copy, halves=range(Q_TILES)):
+            first, last = halves.start * P, halves.stop * P
+            picked = sbuf("m_picked%d_%d" % (r, halves.start), [P, last - first], F32)
+            copy(picked[:], member_sb[r][:].indirect(member_list[:, first // 16 : last // 16]))
+            m_picked.setdefault((r, halves.start), picked)
+
+        def turn_weights(j):
+            nc.vector.scalar_tensor_tensor(
+                out=w_dealt[j][:].rearrange("p t s -> p s t"),
+                in0=a_picked[j][:].rearrange("p (s t) -> p s t", t=PACK),
+                scalar=0.0,
+                in1=h_picked[j][:].rearrange("p (s t) -> p s t", t=PACK),
+                op0=ALU.max,
+                op1=ALU.max,
+            )
+            bank = wide_bank([P, PACK, P])
+            for t in range(PACK):
+                nc.tensor.transpose(bank[:, t, :], w_dealt[j][:, t, :], ident[:])
+            banks.setdefault(("w", j), bank)
+
+        def scale_weights(j):
+            nc.vector.tensor_tensor(
+                out=w_grouped[:, block(j, P), :],
+                in0=banks[("w", j)][:].rearrange("p t q -> p q t"),
+                in1=factor[:].unsqueeze(1).to_broadcast([P, P, PACK]),
+                op=ALU.mult,
+            )
+
+        def turn_values(r):
+            words = v_picked[r][:].bitcast(F32)
+            bank = psum.tile([P, 2, P], F32, name="value_bank", bufs=2)
+            for u in range(2):
+                nc.tensor.transpose(bank[:, u, :], words[:, u : 2 * P : 2], ident[:])
+            banks.setdefault(("v", r), bank)
+
+        def quantize_values(r):
+            v_mx.setdefault(r, mx_tiles("v%d" % r, P))
+            quantize(v_mx[r], v_grouped[r])
+
+        def empty_values(r):
+            v_grouped.setdefault(r, sbuf("v_grouped%d" % r, [P, P, PACK], BF16))
+            nc.scalar.copy(
+                out=v_grouped[r][:].rearrange("p c t -> p (c t)").bitcast(F32).rearrange("p (c u) -> p c u", u=2),
+                in_=banks[("v", r)][:].rearrange("p u c -> p c u"),
+            )
+
+        def mix_values(r):
+            bank = wide_bank([P, Q])
+            product(bank, v_mx[r], slice(None), w_mx[0][:].bitcast(FP8X4), w_mx[1][:])
+            banks.setdefault(("o", r), bank)
+
+        def subtract(r, halves=slice(0, Q_TILES)):
+            nc.vector.tensor_tensor(
+                out=diff[:, halves, r, :],
+                in0=banks[("o", r)][:].rearrange("p (j q) -> p j q", q=P)[:, halves, :],
+                in1=m_picked[(r, halves.start)][:].rearrange("p (j q) -> p j q", q=P),
+                op=ALU.subtract,
+            )
+
+        def store_distance(r, queue):
+            y = sbuf("y%d" % r, [P, Q], F32)
+            nc.scalar.activation(out=y[:].rearrange("p (j q) -> p j q", q=P), in_=diff[:, :, r, :], func=ACT.Abs)
+            queue.dma_start(out=y_rows[r], in_=y[:])
+
+        V, S = vector_copy, scalar_copy
+        vector_copy(*by_lines(q_grouped[:], q_raw[:]))
+        quantize(q_mx, q_grouped)
+        for c in range(4):
+            score_keys(0, c)
+        score_keys(1, 0)
+        score_keys(1, 1)
+        empty_keys(0, 0, S)
+        vector_copy(*by_lines(q2_grouped[:], q2_raw[:]))
+        empty_keys(0, 1, V)
+        empty_keys(0, 2, S)
+        quantize(q2_mx, q2_grouped)
+        empty_keys(0, 3, S)
+        score_keys(1, 2)
+        score_keys(1, 3)
+        empty_keys(1, 0, S)
+        vector_copy(*by_lines(pages_grouped[0][:], pages_raw[0][:]))
+        empty_keys(1, 1, S)
+        empty_keys(1, 2, S)
+        quantize(pages_mx[0], pages_grouped[0])
+        empty_keys(1, 3, S)
+        score_pages(0, 0)
+        score_pages(1, 0)
+        vector_copy(*by_lines(pages_grouped[1][:], pages_raw[1][:]))
+        pick_keys(0, S)
+        quantize(pages_mx[1], pages_grouped[1])
+        empty_pages(0, 0, S)
+        empty_pages(1, 0, S)
+        score_pages(0, 1)
+        score_pages(1, 1)
+        pick_keys(1, V)
+        pick_values(0, S)
+        empty_pages(0, 1, V)
+        empty_pages(1, 1, V)
+        turn_values(0)
+        pick_pages(0, S)
+        pick_pages(1, V)
+        pick_values(1, S)
+        turn_weights(0)
+        turn_weights(1)
+        empty_values(0)
+        scale_weights(0)
+        turn_values(1)
+        pick_values(2, S)
+        scale_weights(1)
+        quantize_values(0)
+        quantize(w_mx, w_grouped)
+        empty_values(1)
+        turn_values(2)
+        pick_values(3, V)
+        quantize_values(1)
+        mix_values(0)
+        mix_values(1)
+        pick_members(0, S)
+        empty_values(2)
+        turn_values(3)
+        subtract(0)
+        quantize_values(2)
+        mix_values(2)
+        pick_members(1, S)
+        empty_values(3)
+        subtract(1)
+        store_distance(0, nc.sync)
+        pick_members(2, V)
+        quantize_values(3)
+        mix_values(3)
+        subtract(2)
+        store_distance(1, nc.sync)
+        pick_members(3, V, range(0, 1))
+        pick_members(3, S, range(1, 2))
+        store_distance(2, nc.sync)
+        subtract(3, slice(0, 1))
+        subtract(3, slice(1, 2))
+        grouped0, planes0 = by_lines(y_grouped[0][:], diff[:, 0, :, :])
+        nc.scalar.activation(out=grouped0, in_=planes0, func=ACT.Abs)
+        signed = diff[:, 1, :, :].rearrange("p r q -> p q r")
+        nc.vector.scalar_tensor_tensor(out=y_grouped[1][:], in0=signed, scalar=-1.0, in1=signed, op0=ALU.mult, op1=ALU.max)
+        store_distance(3, nc.scalar)
+        for j in range(Q_TILES):
+            quantize(y_mx, y_grouped[j], block(j, P))
+        y_codes, y_scales = y_mx
+        nc.sync.dma_start(out=out_1[0].rearrange("p c r -> p (c r)").bitcast(I32), in_=y_codes[:].bitcast(I32))
+        for quad in range(4):
+            queue = nc.scalar if quad % 2 else nc.sync
+            queue.dma_start(
+                out=out_2[0, 4 * quad : 4 * quad + 4, :].bitcast(I32),
+                in_=y_scales[32 * quad : 32 * quad + 4, :].bitcast(I32),
+            )

@@ -89,19 +89,16 @@ def tile_attend_crosslarger_distanceout_lean_pl_kernel(
         nc.sync.dma_start(out=q_raw[:], in_=query.rearrange("(p t) q -> p t q", t=PACK))
         key_words = sbuf("key_words", [P, 2 * T], U8)
         nc.sync.dma_start(out=key_words[:].bitcast(I32), in_=keys_words[0].bitcast(I32))
-        for quad in range(4):
-            nc.sync.dma_start(
-                out=key_scales[32 * quad : 32 * quad + 4, :].bitcast(I32),
-                in_=keys_scales[0, 4 * quad : 4 * quad + 4, :].bitcast(I32),
-            )
-        token_list = lists.tile([P, I // 16], U16, name="token_list")
-        nc.sync.dma_start(token_list[:], offs)
+        for row in range(4):
+            nc.sync.dma_start(out=key_scales[row:P:32, :].bitcast(I32), in_=keys_scales[0, row:16:4, :].bitcast(I32))
         q2_raw = sbuf("q2_raw", [P, PACK, Q], F32)
         nc.sync.dma_start(out=q2_raw[:], in_=query2.rearrange("(p t) q -> p t q", t=PACK))
         pages_rows = pages.rearrange("(p t) z -> p t z", t=PACK)
         pages_raw = [sbuf("pages_raw%d" % c, [P, PACK, BANK], F32) for c in range(Z // BANK)]
-        for c in range(Z // BANK):
-            nc.sync.dma_start(out=pages_raw[c][:], in_=pages_rows[:, :, block(c, BANK)])
+        nc.sync.dma_start(out=pages_raw[0][:], in_=pages_rows[:, :, block(0, BANK)])
+        token_list = lists.tile([P, I // 16], U16, name="token_list")
+        nc.sync.dma_start(token_list[:], offs)
+        nc.sync.dma_start(out=pages_raw[1][:], in_=pages_rows[:, :, block(1, BANK)])
         page_list = lists.tile([P, I // 16], U16, name="page_list")
         nc.sync.dma_start(page_list[:], offs2)
         member_list = lists.tile([P, Q // 16], U16, name="member_list")
@@ -127,7 +124,7 @@ def tile_attend_crosslarger_distanceout_lean_pl_kernel(
         h_sb = [sbuf("h%d" % j, [P, Z], F32) for j in range(Q_TILES)]
         a_picked = {}
         h_picked = {}
-        w_dealt = [sbuf("w_dealt%d" % j, [P, PACK, P], F32) for j in range(Q_TILES)]
+        w_dealt = [sbuf("w_dealt%d" % j, [P, 2, 2 * P], F32) for j in range(Q_TILES)]
         w_grouped = sbuf("w_grouped", [P, Q, PACK], BF16)
         v_picked = [sbuf("v_picked%d" % r, [P, I], BF16) for r in range(PACK)]
         v_grouped = {}
@@ -174,25 +171,25 @@ def tile_attend_crosslarger_distanceout_lean_pl_kernel(
             m_picked.setdefault((r, halves.start), picked)
 
         def turn_weights(j):
-            nc.vector.scalar_tensor_tensor(
-                out=w_dealt[j][:].rearrange("p t s -> p s t"),
-                in0=a_picked[j][:].rearrange("p (s t) -> p s t", t=PACK),
-                scalar=0.0,
-                in1=h_picked[j][:].rearrange("p (s t) -> p s t", t=PACK),
-                op0=ALU.max,
-                op1=ALU.max,
+            nc.vector.tensor_tensor(
+                out=w_dealt[j][:].rearrange("p u (s e) -> p s u e", e=2),
+                in0=a_picked[j][:].rearrange("p (s u e) -> p s u e", u=2, e=2),
+                in1=h_picked[j][:].rearrange("p (s u e) -> p s u e", u=2, e=2),
+                op=ALU.max,
             )
             bank = wide_bank([P, PACK, P])
             for t in range(PACK):
-                nc.tensor.transpose(bank[:, t, :], w_dealt[j][:, t, :], ident[:])
+                nc.tensor.transpose(bank[:, t, :], w_dealt[j][:, t // 2, t % 2 : 2 * P : 2], ident[:])
             banks.setdefault(("w", j), bank)
 
         def scale_weights(j):
-            nc.vector.tensor_tensor(
+            nc.vector.scalar_tensor_tensor(
                 out=w_grouped[:, block(j, P), :],
                 in0=banks[("w", j)][:].rearrange("p t q -> p q t"),
+                scalar=0.0,
                 in1=factor[:].unsqueeze(1).to_broadcast([P, P, PACK]),
-                op=ALU.mult,
+                op0=ALU.max,
+                op1=ALU.mult,
             )
 
         def turn_values(r):
@@ -313,9 +310,6 @@ def tile_attend_crosslarger_distanceout_lean_pl_kernel(
             quantize(y_mx, y_grouped[j], block(j, P))
         y_codes, y_scales = y_mx
         nc.sync.dma_start(out=out_1[0].rearrange("p c r -> p (c r)").bitcast(I32), in_=y_codes[:].bitcast(I32))
-        for quad in range(4):
-            queue = nc.scalar if quad % 2 else nc.sync
-            queue.dma_start(
-                out=out_2[0, 4 * quad : 4 * quad + 4, :].bitcast(I32),
-                in_=y_scales[32 * quad : 32 * quad + 4, :].bitcast(I32),
-            )
+        for row in range(4):
+            queue = nc.scalar if row % 2 else nc.sync
+            queue.dma_start(out=out_2[0, row:16:4, :].bitcast(I32), in_=y_scales[row:P:32, :].bitcast(I32))

@@ -21,6 +21,8 @@ P = 128
 PACK = 4
 BANK = 512
 Q_TILES = Q // P
+KEY_LOADS = 2
+KEY_COLS = T // KEY_LOADS
 
 
 def tile_attend_crosslarger_distanceout_lean_pl_kernel(
@@ -32,17 +34,14 @@ def tile_attend_crosslarger_distanceout_lean_pl_kernel(
         sb = ctx.enter_context(tc.tile_pool(name="sb", bufs=1))
         psum = ctx.enter_context(tc.psum_pool(name="psum", bufs=1))
 
-        over = {"a_picked1": "pages_grouped1", "h_picked0": "vals0", "v_grouped0": "vals1", "v_grouped1": "vals2", "v1_codes": "vals3", "v_grouped2": "member0", "v_grouped3": "member1", "y0": "m_picked1_0", "v3_codes": "member2", "y2": "member3"}
-
-        def sbuf(name, shape, dtype):
-            return sb.tile(shape, dtype, name=name, tag=over.get(name, name), align_bytes=64)
-
-        def clock(name, ap):
-            c = sbuf(name, [P, 1], F32)
-            nc.gpsimd.tensor_copy(out=c[:], in_=ap)
+        def sbuf(name, shape, dtype, over=None):
+            return sb.tile(shape, dtype, name=name, tag=over or name, align_bytes=64)
 
         def wide_bank(shape):
             return psum.tile(shape, F32, name="wide_bank", bufs=6)
+
+        def value_bank(shape):
+            return psum.tile(shape, F32, name="value_bank", bufs=2)
 
         def vector_copy(out, in_):
             nc.vector.tensor_copy(out=out, in_=in_)
@@ -56,8 +55,8 @@ def tile_attend_crosslarger_distanceout_lean_pl_kernel(
                 planes.rearrange("p t (c i) -> p c t i", i=4),
             )
 
-        def mx_tiles(name, width):
-            return sbuf(name + "_codes", [P, width], U32), sbuf(name + "_scales", [P, width], U8)
+        def mx_tiles(name, width, over=None):
+            return sbuf(name + "_codes", [P, width], U32, over), sbuf(name + "_scales", [P, width], U8)
 
         def quantize(operand, grouped, cols=slice(None)):
             codes, scales = operand
@@ -87,10 +86,11 @@ def tile_attend_crosslarger_distanceout_lean_pl_kernel(
 
         q_raw = sbuf("q_raw", [P, PACK, Q], F32)
         nc.sync.dma_start(out=q_raw[:], in_=query.rearrange("(p t) q -> p t q", t=PACK))
-        key_words = sbuf("key_words", [P, 2 * T], U8)
-        nc.sync.dma_start(out=key_words[:].bitcast(I32), in_=keys_words[0].bitcast(I32))
+        key_words = [sbuf("key_words%d" % n, [P, 2 * KEY_COLS], U8) for n in range(KEY_LOADS)]
+        nc.sync.dma_start(out=key_words[0][:].bitcast(I32), in_=keys_words[0, :, block(0, 2 * KEY_COLS)].bitcast(I32))
         for row in range(4):
             nc.sync.dma_start(out=key_scales[row:P:32, :].bitcast(I32), in_=keys_scales[0, row:16:4, :].bitcast(I32))
+        nc.sync.dma_start(out=key_words[1][:].bitcast(I32), in_=keys_words[0, :, block(1, 2 * KEY_COLS)].bitcast(I32))
         q2_raw = sbuf("q2_raw", [P, PACK, Q], F32)
         nc.sync.dma_start(out=q2_raw[:], in_=query2.rearrange("(p t) q -> p t q", t=PACK))
         pages_rows = pages.rearrange("(p t) z -> p t z", t=PACK)
@@ -114,197 +114,176 @@ def tile_attend_crosslarger_distanceout_lean_pl_kernel(
         for r in range(PACK):
             nc.sync.dma_start(out=member_sb[r][:], in_=member_rows[r])
 
-        q_grouped = sbuf("q_grouped", [P, Q, PACK], BF16)
-        q2_grouped = sbuf("q2_grouped", [P, Q, PACK], BF16)
-        pages_grouped = [sbuf("pages_grouped%d" % c, [P, BANK, PACK], BF16) for c in range(Z // BANK)]
         q_mx, q2_mx, w_mx, y_mx = (mx_tiles(name, Q) for name in ("q", "q2", "w", "y"))
-        pages_mx = [mx_tiles("pages%d" % c, BANK) for c in range(Z // BANK)]
-        v_mx = {}
         a_sb = [sbuf("a%d" % j, [P, T], F32) for j in range(Q_TILES)]
         h_sb = [sbuf("h%d" % j, [P, Z], F32) for j in range(Q_TILES)]
-        a_picked = {}
-        h_picked = {}
-        w_dealt = [sbuf("w_dealt%d" % j, [P, 2, 2 * P], F32) for j in range(Q_TILES)]
         w_grouped = sbuf("w_grouped", [P, Q, PACK], BF16)
-        v_picked = [sbuf("v_picked%d" % r, [P, I], BF16) for r in range(PACK)]
-        v_grouped = {}
-        m_picked = {}
         diff = sbuf("diff", [P, Q_TILES, PACK, P], F32)
-        y_grouped = [sbuf("y_grouped%d" % j, [P, P, PACK], BF16) for j in range(Q_TILES)]
         y_rows = out_0.rearrange("(p r) q -> r p q", r=PACK)
-        banks = {}
+
+        def regroup(name, planes, width, copy):
+            grouped = sbuf(name, [P, width, PACK], BF16)
+            copy(*by_lines(grouped[:], planes))
+            return grouped
 
         def score_keys(j, c):
             bank = wide_bank([P, BANK])
-            product(
-                bank, q_mx, block(j, P), key_words[:, block(c, 2 * BANK)].bitcast(FP4X4), key_scales[:, block(c, BANK)]
-            )
-            banks.setdefault(("a", j, c), bank)
+            load, place = divmod(c, KEY_COLS // BANK)
+            words = key_words[load][:, block(place, 2 * BANK)]
+            product(bank, q_mx, block(j, P), words.bitcast(FP4X4), key_scales[:, block(c, BANK)])
+            return bank
 
-        def empty_keys(j, c, copy):
-            copy(a_sb[j][:, block(c, BANK)], banks[("a", j, c)][:])
-
-        def score_pages(j, c):
+        def score_pages(j, pages_mx):
             bank = wide_bank([P, BANK])
-            codes, scales = pages_mx[c]
-            product(bank, q2_mx, block(j, P), codes[:].bitcast(FP8X4), scales[:])
-            banks.setdefault(("h", j, c), bank)
+            product(bank, q2_mx, block(j, P), pages_mx[0][:].bitcast(FP8X4), pages_mx[1][:])
+            return bank
 
-        def empty_pages(j, c, copy):
-            copy(h_sb[j][:, block(c, BANK)], banks[("h", j, c)][:])
+        def pick(name, window, offsets, count, dtype, copy, over=None):
+            picked = sbuf(name, [P, count], dtype, over)
+            copy(picked[:], window[:].indirect(offsets))
+            return picked
 
-        def pick_keys(j, copy):
-            a_picked.setdefault(j, sbuf("a_picked%d" % j, [P, I], F32))
-            copy(a_picked[j][:], a_sb[j][:].indirect(token_list[:]))
-
-        def pick_pages(j, copy):
-            h_picked.setdefault(j, sbuf("h_picked%d" % j, [P, I], F32))
-            copy(h_picked[j][:], h_sb[j][:].indirect(page_list[:]))
-
-        def pick_values(r, copy):
-            copy(v_picked[r][:], vals_sb[r][:].indirect(token_list[:]))
-
-        def pick_members(r, copy, halves=range(Q_TILES)):
-            first, last = halves.start * P, halves.stop * P
-            picked = sbuf("m_picked%d_%d" % (r, halves.start), [P, last - first], F32)
-            copy(picked[:], member_sb[r][:].indirect(member_list[:, first // 16 : last // 16]))
-            m_picked.setdefault((r, halves.start), picked)
-
-        def turn_weights(j):
-            nc.vector.tensor_tensor(
-                out=w_dealt[j][:].rearrange("p u (s e) -> p s u e", e=2),
-                in0=a_picked[j][:].rearrange("p (s u e) -> p s u e", u=2, e=2),
-                in1=h_picked[j][:].rearrange("p (s u e) -> p s u e", u=2, e=2),
-                op=ALU.max,
+        def turn_weights(j, from_keys, from_pages, over=None):
+            dealt = sbuf("w_dealt%d" % j, [P, PACK, P], F32, over)
+            nc.vector.scalar_tensor_tensor(
+                out=dealt[:].rearrange("p t s -> p s t"),
+                in0=from_keys[:].rearrange("p (s t) -> p s t", t=PACK),
+                scalar=0.0,
+                in1=from_pages[:].rearrange("p (s t) -> p s t", t=PACK),
+                op0=ALU.max,
+                op1=ALU.max,
             )
             bank = wide_bank([P, PACK, P])
             for t in range(PACK):
-                nc.tensor.transpose(bank[:, t, :], w_dealt[j][:, t // 2, t % 2 : 2 * P : 2], ident[:])
-            banks.setdefault(("w", j), bank)
+                nc.tensor.transpose(bank[:, t, :], dealt[:, t, :], ident[:])
+            return bank
 
-        def scale_weights(j):
-            nc.vector.scalar_tensor_tensor(
+        def scale_weights(j, bank):
+            nc.vector.tensor_tensor(
                 out=w_grouped[:, block(j, P), :],
-                in0=banks[("w", j)][:].rearrange("p t q -> p q t"),
-                scalar=0.0,
+                in0=bank[:].rearrange("p t q -> p q t"),
                 in1=factor[:].unsqueeze(1).to_broadcast([P, P, PACK]),
-                op0=ALU.max,
-                op1=ALU.mult,
+                op=ALU.mult,
             )
 
-        def turn_values(r):
-            words = v_picked[r][:].bitcast(F32)
-            bank = psum.tile([P, 2, P], F32, name="value_bank", bufs=2)
+        def turn_values(picked, bank):
+            words = picked[:].bitcast(F32)
             for u in range(2):
                 nc.tensor.transpose(bank[:, u, :], words[:, u : 2 * P : 2], ident[:])
-            banks.setdefault(("v", r), bank)
 
-        def quantize_values(r):
-            v_mx.setdefault(r, mx_tiles("v%d" % r, P))
-            quantize(v_mx[r], v_grouped[r])
-
-        def empty_values(r):
-            v_grouped.setdefault(r, sbuf("v_grouped%d" % r, [P, P, PACK], BF16))
+        def regroup_values(name, bank, over=None):
+            planes = bank.shape[1]
+            grouped = sbuf(name, [P, planes * P, PACK], BF16, over)
+            words = grouped[:].rearrange("p c t -> p (c t)").bitcast(F32)
             nc.scalar.copy(
-                out=v_grouped[r][:].rearrange("p c t -> p (c t)").bitcast(F32).rearrange("p (c u) -> p c u", u=2),
-                in_=banks[("v", r)][:].rearrange("p u c -> p c u"),
+                out=words.rearrange("p (r c u) -> p r c u", r=planes, u=2), in_=bank[:].rearrange("p r u c -> p r c u")
             )
+            return grouped
 
-        def mix_values(r):
+        def quantize_values(name, grouped, over):
+            operand = mx_tiles(name, grouped.shape[1], over)
+            quantize(operand, grouped)
+            return operand
+
+        def mix_values(v_mx, place):
             bank = wide_bank([P, Q])
-            product(bank, v_mx[r], slice(None), w_mx[0][:].bitcast(FP8X4), w_mx[1][:])
-            banks.setdefault(("o", r), bank)
+            product(bank, v_mx, block(place, P), w_mx[0][:].bitcast(FP8X4), w_mx[1][:])
+            return bank
 
-        def subtract(r, halves=slice(0, Q_TILES)):
+        def subtract(r, bank, picked, tiles=slice(0, Q_TILES)):
             nc.vector.tensor_tensor(
-                out=diff[:, halves, r, :],
-                in0=banks[("o", r)][:].rearrange("p (j q) -> p j q", q=P)[:, halves, :],
-                in1=m_picked[(r, halves.start)][:].rearrange("p (j q) -> p j q", q=P),
+                out=diff[:, tiles, r, :],
+                in0=bank[:].rearrange("p (j q) -> p j q", q=P)[:, tiles, :],
+                in1=picked[:].rearrange("p (j q) -> p j q", q=P),
                 op=ALU.subtract,
             )
 
-        def store_distance(r, queue):
-            y = sbuf("y%d" % r, [P, Q], F32)
+        def store_distance(r, queue, over=None):
+            y = sbuf("y%d" % r, [P, Q], F32, over)
             nc.scalar.activation(out=y[:].rearrange("p (j q) -> p j q", q=P), in_=diff[:, :, r, :], func=ACT.Abs)
             queue.dma_start(out=y_rows[r], in_=y[:])
 
-        V, S = vector_copy, scalar_copy
-        vector_copy(*by_lines(q_grouped[:], q_raw[:]))
-        quantize(q_mx, q_grouped)
-        for c in range(4):
-            score_keys(0, c)
-        score_keys(1, 0)
-        score_keys(1, 1)
-        empty_keys(0, 0, S)
-        vector_copy(*by_lines(q2_grouped[:], q2_raw[:]))
-        empty_keys(0, 1, V)
-        empty_keys(0, 2, S)
+        q_grouped = [
+            regroup("q_grouped%d" % j, q_raw[:, :, block(j, P)], P, (vector_copy, scalar_copy)[j]) for j in range(Q_TILES)
+        ]
+        for j in range(Q_TILES):
+            quantize(q_mx, q_grouped[j], block(j, P))
+        a_banks = [score_keys(0, c) for c in range(T // BANK)]
+        scalar_copy(a_sb[0][:, block(0, BANK)], a_banks[0][:])
+        vector_copy(a_sb[0][:, block(1, BANK)], a_banks[1][:])
+        q2_grouped = regroup("q2_grouped", q2_raw[:], Q, vector_copy)
+        scalar_copy(a_sb[0][:, block(2, BANK)], a_banks[2][:])
+        scalar_copy(a_sb[0][:, block(3, BANK)], a_banks[3][:])
         quantize(q2_mx, q2_grouped)
-        empty_keys(0, 3, S)
-        score_keys(1, 2)
-        score_keys(1, 3)
-        empty_keys(1, 0, S)
-        vector_copy(*by_lines(pages_grouped[0][:], pages_raw[0][:]))
-        empty_keys(1, 1, S)
-        empty_keys(1, 2, S)
-        quantize(pages_mx[0], pages_grouped[0])
-        empty_keys(1, 3, S)
-        score_pages(0, 0)
-        score_pages(1, 0)
-        vector_copy(*by_lines(pages_grouped[1][:], pages_raw[1][:]))
-        pick_keys(0, S)
-        quantize(pages_mx[1], pages_grouped[1])
-        empty_pages(0, 0, S)
-        empty_pages(1, 0, S)
-        score_pages(0, 1)
-        score_pages(1, 1)
-        pick_keys(1, V)
-        pick_values(0, S)
-        empty_pages(0, 1, V)
-        empty_pages(1, 1, V)
-        turn_values(0)
-        pick_pages(0, S)
-        pick_pages(1, V)
-        pick_values(1, S)
-        turn_weights(0)
-        turn_weights(1)
-        empty_values(0)
-        scale_weights(0)
-        turn_values(1)
-        pick_values(2, S)
-        scale_weights(1)
-        quantize_values(0)
+        for c in range(T // BANK):
+            scalar_copy(a_sb[1][:, block(c, BANK)], score_keys(1, c)[:])
+
+        pages_grouped0 = regroup("pages_grouped0", pages_raw[0][:], BANK, vector_copy)
+        pages_mx0 = quantize_values("pages0", pages_grouped0, None)
+        h_banks0 = [score_pages(j, pages_mx0) for j in range(Q_TILES)]
+        a_picked0 = pick("a_picked0", a_sb[0], token_list[:], I, F32, scalar_copy)
+        pages_grouped1 = regroup("pages_grouped1", pages_raw[1][:], BANK, vector_copy)
+        pages_mx1 = quantize_values("pages1", pages_grouped1, None)
+        for j in range(Q_TILES):
+            scalar_copy(h_sb[j][:, block(0, BANK)], h_banks0[j][:])
+        h_banks1 = [score_pages(j, pages_mx1) for j in range(Q_TILES)]
+        a_picked1 = pick("a_picked1", a_sb[1], token_list[:], I, F32, vector_copy, over="pages_grouped1")
+        for j in range(Q_TILES):
+            scalar_copy(h_sb[j][:, block(1, BANK)], h_banks1[j][:])
+
+        h_picked0 = pick("h_picked0", h_sb[0], page_list[:], I, F32, vector_copy)
+        v_picked0 = pick("v_picked0", vals_sb[0], token_list[:], I, BF16, scalar_copy, over="pages1_codes")
+        h_picked1 = pick("h_picked1", h_sb[1], page_list[:], I, F32, vector_copy)
+        w_bank0 = turn_weights(0, a_picked0, h_picked0, over="h1")
+        v_bank01 = value_bank([P, 2, 2, P])
+        turn_values(v_picked0, v_bank01[:, 0])
+        v_picked1 = pick("v_picked1", vals_sb[1], token_list[:], I, BF16, scalar_copy)
+        w_bank1 = turn_weights(1, a_picked1, h_picked1)
+        scale_weights(0, w_bank0)
+        turn_values(v_picked1, v_bank01[:, 1])
+        v_picked2 = pick("v_picked2", vals_sb[2], token_list[:], I, BF16, scalar_copy)
+        scale_weights(1, w_bank1)
         quantize(w_mx, w_grouped)
-        empty_values(1)
-        turn_values(2)
-        pick_values(3, V)
-        quantize_values(1)
-        mix_values(0)
-        mix_values(1)
-        pick_members(0, S)
-        empty_values(2)
-        turn_values(3)
-        subtract(0)
-        quantize_values(2)
-        mix_values(2)
-        pick_members(1, S)
-        empty_values(3)
-        subtract(1)
-        store_distance(0, nc.sync)
-        pick_members(2, V)
-        quantize_values(3)
-        mix_values(3)
-        subtract(2)
+        v_bank2 = value_bank([P, 1, 2, P])
+        turn_values(v_picked2, v_bank2[:, 0])
+        v_grouped01 = regroup_values("v_grouped01", v_bank01, over="vals2")
+        v_picked3 = pick("v_picked3", vals_sb[3], token_list[:], I, BF16, vector_copy)
+        v_mx01 = quantize_values("v01", v_grouped01, over="vals3")
+        o_bank0 = mix_values(v_mx01, 0)
+        o_bank1 = mix_values(v_mx01, 1)
+        v_grouped2 = regroup_values("v_grouped2", v_bank2)
+        m_picked0 = pick("m_picked0", member_sb[0], member_list[:], Q, F32, vector_copy)
+        v_bank3 = value_bank([P, 1, 2, P])
+        turn_values(v_picked3, v_bank3[:, 0])
+        v_mx2 = quantize_values("v2", v_grouped2, over="member0")
+        o_bank2 = mix_values(v_mx2, 0)
+        subtract(0, o_bank0, m_picked0)
+        m_picked1 = pick("m_picked1", member_sb[1], member_list[:], Q, F32, scalar_copy)
+        v_grouped3 = regroup_values("v_grouped3", v_bank3, over="member1")
+        subtract(1, o_bank1, m_picked1)
+        m_picked2 = pick("m_picked2", member_sb[2], member_list[:], Q, F32, vector_copy)
+        v_mx3 = quantize_values("v3", v_grouped3, over="member2")
+        o_bank3 = mix_values(v_mx3, 0)
+        store_distance(0, nc.sync, over="m_picked1")
+        subtract(2, o_bank2, m_picked2)
         store_distance(1, nc.sync)
-        pick_members(3, V, range(0, 1))
-        pick_members(3, S, range(1, 2))
-        store_distance(2, nc.sync)
-        subtract(3, slice(0, 1))
-        subtract(3, slice(1, 2))
-        grouped0, planes0 = by_lines(y_grouped[0][:], diff[:, 0, :, :])
-        nc.scalar.activation(out=grouped0, in_=planes0, func=ACT.Abs)
+
+        m_picked3 = [
+            pick(
+                "m_picked3_%d" % j, member_sb[3], member_list[:, block(j, P // 16)], P, F32, (vector_copy, scalar_copy)[j]
+            )
+            for j in range(Q_TILES)
+        ]
+        store_distance(2, nc.sync, over="member3")
+        for j in range(Q_TILES):
+            subtract(3, o_bank3, m_picked3[j], block(j, 1))
+        y_grouped = [sbuf("y_grouped%d" % j, [P, P, PACK], BF16) for j in range(Q_TILES)]
+        grouped_lines, signed_lines = by_lines(y_grouped[0][:], diff[:, 0, :, :])
+        nc.scalar.activation(out=grouped_lines, in_=signed_lines, func=ACT.Abs)
         signed = diff[:, 1, :, :].rearrange("p r q -> p q r")
-        nc.vector.scalar_tensor_tensor(out=y_grouped[1][:], in0=signed, scalar=-1.0, in1=signed, op0=ALU.mult, op1=ALU.max)
+        nc.vector.scalar_tensor_tensor(
+            out=y_grouped[1][:], in0=signed, scalar=-1.0, in1=signed, op0=ALU.mult, op1=ALU.max
+        )
         store_distance(3, nc.scalar)
         for j in range(Q_TILES):
             quantize(y_mx, y_grouped[j], block(j, P))

@@ -51,8 +51,8 @@ def tile_attend_crosslarger_distanceout_lean_pl_kernel(
 
         def by_lines(grouped, planes):
             return (
-                grouped.rearrange("p (c i) t -> p c t i", i=4),
-                planes.rearrange("p t (c i) -> p c t i", i=4),
+                grouped.rearrange("p (c i) t -> p c t i", i=2),
+                planes.rearrange("p t (c i) -> p c t i", i=2),
             )
 
         def mx_tiles(name, width, over=None):

from contextlib import ExitStack

import concourse.mybir as mybir
from concourse.masks import make_identity

D, T, I, Q, E, Z, M = 512, 2048, 512, 256, 512, 1024, 1024
FLOPS = 2 * Q * D * T + 2 * Q * D * Z + 2 * E * I * Q

F32 = mybir.dt.float32
BF16 = mybir.dt.bfloat16
I32 = mybir.dt.int32
U32 = mybir.dt.uint32
U16 = mybir.dt.uint16
U8 = mybir.dt.uint8
FP8X4 = mybir.dt.float8_e4m3fn_x4
FP4X4 = mybir.dt.float4_e2m1fn_x4
ALU = mybir.AluOpType
ACT = mybir.ActivationFunctionType

P = 128
PACK = 4
BANK = 512
Q_TILES = Q // P
KEY_LOADS = 2
KEY_COLS = T // KEY_LOADS


def tile_attend_crosslarger_distanceout_lean_pl_kernel(
    tc, query, query2, keys_words, keys_scales, pages, slot_factor, vals, member, offs, offs2, offs3, out_0, out_1, out_2
):
    nc = tc.nc
    with ExitStack() as ctx:
        lists = ctx.enter_context(tc.tile_pool(name="lists", bufs=1))
        sb = ctx.enter_context(tc.tile_pool(name="sb", bufs=1))
        psum = ctx.enter_context(tc.psum_pool(name="psum", bufs=1))

        def sbuf(name, shape, dtype, over=None):
            return sb.tile(shape, dtype, name=name, tag=over or name, align_bytes=64)

        def wide_bank(shape):
            return psum.tile(shape, F32, name="wide_bank", bufs=6)

        def value_bank(shape):
            return psum.tile(shape, F32, name="value_bank", bufs=2)

        def vector_copy(out, in_):
            nc.vector.tensor_copy(out=out, in_=in_)

        def scalar_copy(out, in_):
            nc.scalar.activation(out=out, in_=in_, func=ACT.Copy)

        def by_lines(grouped, planes):
            return (
                grouped.rearrange("p (c i) t -> p c t i", i=2),
                planes.rearrange("p t (c i) -> p c t i", i=2),
            )

        def mx_tiles(name, width, over=None):
            return sbuf(name + "_codes", [P, width], U32, over), sbuf(name + "_scales", [P, width], U8)

        def quantize(operand, grouped, cols=slice(None)):
            codes, scales = operand
            nc.vector.quantize_mx(
                out=codes[:, cols].bitcast(FP8X4), scales=scales[:, cols], in_=grouped[:].rearrange("p c t -> p (c t)")
            )

        def product(bank, stationary, cols, moving_codes, moving_scales):
            codes, scales = stationary
            nc.tensor.matmul_mx(
                out=bank[:],
                lhsT=codes[:, cols].bitcast(FP8X4),
                lhsT_scale=scales[:, cols],
                rhs=moving_codes,
                rhs_scale=moving_scales,
                start=True,
                stop=True,
            )

        def block(n, width):
            return slice(n * width, (n + 1) * width)

        key_scales = sbuf("key_scales", [P, T], U8)
        nc.vector.memset(key_scales[:].bitcast(I32), 0)
        ident = sbuf("ident", [P, P], F32)
        make_identity(nc, ident[:])

        q_raw = sbuf("q_raw", [P, PACK, Q], F32)
        nc.sync.dma_start(out=q_raw[:], in_=query.rearrange("(p t) q -> p t q", t=PACK))
        key_words = [sbuf("key_words%d" % n, [P, 2 * KEY_COLS], U8) for n in range(KEY_LOADS)]
        nc.sync.dma_start(out=key_words[0][:].bitcast(I32), in_=keys_words[0, :, block(0, 2 * KEY_COLS)].bitcast(I32))
        for row in range(4):
            nc.sync.dma_start(out=key_scales[row:P:32, :].bitcast(I32), in_=keys_scales[0, row:16:4, :].bitcast(I32))
        nc.sync.dma_start(out=key_words[1][:].bitcast(I32), in_=keys_words[0, :, block(1, 2 * KEY_COLS)].bitcast(I32))
        q2_raw = sbuf("q2_raw", [P, PACK, Q], F32)
        nc.sync.dma_start(out=q2_raw[:], in_=query2.rearrange("(p t) q -> p t q", t=PACK))
        pages_rows = pages.rearrange("(p t) z -> p t z", t=PACK)
        pages_raw = [sbuf("pages_raw%d" % c, [P, PACK, BANK], F32) for c in range(Z // BANK)]
        nc.sync.dma_start(out=pages_raw[0][:], in_=pages_rows[:, :, block(0, BANK)])
        token_list = lists.tile([P, I // 16], U16, name="token_list")
        nc.sync.dma_start(token_list[:], offs)
        nc.sync.dma_start(out=pages_raw[1][:], in_=pages_rows[:, :, block(1, BANK)])
        page_list = lists.tile([P, I // 16], U16, name="page_list")
        nc.sync.dma_start(page_list[:], offs2)
        member_list = lists.tile([P, Q // 16], U16, name="member_list")
        nc.sync.dma_start(member_list[:], offs3)
        factor = sbuf("factor", [P, PACK], F32)
        nc.sync.dma_start(out=factor[:], in_=slot_factor.rearrange("o (p t) -> (o p) t", t=PACK))
        vals_rows = vals.rearrange("(p r) t -> r p t", r=PACK)
        vals_sb = [sbuf("vals%d" % r, [P, T], F32) for r in range(PACK)]
        for r in range(PACK):
            nc.sync.dma_start(out=vals_sb[r][:], in_=vals_rows[r])
        member_rows = member.rearrange("(p r) m -> r p m", r=PACK)
        member_sb = [sbuf("member%d" % r, [P, M], F32) for r in range(PACK)]
        for r in range(PACK):
            nc.sync.dma_start(out=member_sb[r][:], in_=member_rows[r])

        q_mx, q2_mx, w_mx, y_mx = (mx_tiles(name, Q) for name in ("q", "q2", "w", "y"))
        a_sb = [sbuf("a%d" % j, [P, T], F32) for j in range(Q_TILES)]
        h_sb = [sbuf("h%d" % j, [P, Z], F32) for j in range(Q_TILES)]
        w_grouped = sbuf("w_grouped", [P, Q, PACK], BF16)
        diff = sbuf("diff", [P, Q_TILES, PACK, P], F32)
        y_rows = out_0.rearrange("(p r) q -> r p q", r=PACK)

        def regroup(name, planes, width, copy):
            grouped = sbuf(name, [P, width, PACK], BF16)
            copy(*by_lines(grouped[:], planes))
            return grouped

        def score_keys(j, c):
            bank = wide_bank([P, BANK])
            load, place = divmod(c, KEY_COLS // BANK)
            words = key_words[load][:, block(place, 2 * BANK)]
            product(bank, q_mx, block(j, P), words.bitcast(FP4X4), key_scales[:, block(c, BANK)])
            return bank

        def score_pages(j, pages_mx):
            bank = wide_bank([P, BANK])
            product(bank, q2_mx, block(j, P), pages_mx[0][:].bitcast(FP8X4), pages_mx[1][:])
            return bank

        def pick(name, window, offsets, count, dtype, copy, over=None):
            picked = sbuf(name, [P, count], dtype, over)
            copy(picked[:], window[:].indirect(offsets))
            return picked

        def turn_weights(j, from_keys, from_pages, over=None):
            dealt = sbuf("w_dealt%d" % j, [P, PACK, P], F32, over)
            nc.vector.scalar_tensor_tensor(
                out=dealt[:].rearrange("p t s -> p s t"),
                in0=from_keys[:].rearrange("p (s t) -> p s t", t=PACK),
                scalar=0.0,
                in1=from_pages[:].rearrange("p (s t) -> p s t", t=PACK),
                op0=ALU.max,
                op1=ALU.max,
            )
            bank = wide_bank([P, PACK, P])
            for t in range(PACK):
                nc.tensor.transpose(bank[:, t, :], dealt[:, t, :], ident[:])
            return bank

        def scale_weights(j, bank):
            nc.vector.tensor_tensor(
                out=w_grouped[:, block(j, P), :],
                in0=bank[:].rearrange("p t q -> p q t"),
                in1=factor[:].unsqueeze(1).to_broadcast([P, P, PACK]),
                op=ALU.mult,
            )

        def turn_values(picked, bank):
            words = picked[:].bitcast(F32)
            for u in range(2):
                nc.tensor.transpose(bank[:, u, :], words[:, u : 2 * P : 2], ident[:])

        def regroup_values(name, bank, over=None):
            planes = bank.shape[1]
            grouped = sbuf(name, [P, planes * P, PACK], BF16, over)
            words = grouped[:].rearrange("p c t -> p (c t)").bitcast(F32)
            nc.scalar.copy(
                out=words.rearrange("p (r c u) -> p r c u", r=planes, u=2), in_=bank[:].rearrange("p r u c -> p r c u")
            )
            return grouped

        def quantize_values(name, grouped, over):
            operand = mx_tiles(name, grouped.shape[1], over)
            quantize(operand, grouped)
            return operand

        def mix_values(v_mx, place):
            bank = wide_bank([P, Q])
            product(bank, v_mx, block(place, P), w_mx[0][:].bitcast(FP8X4), w_mx[1][:])
            return bank

        def subtract(r, bank, picked, tiles=slice(0, Q_TILES)):
            nc.vector.tensor_tensor(
                out=diff[:, tiles, r, :],
                in0=bank[:].rearrange("p (j q) -> p j q", q=P)[:, tiles, :],
                in1=picked[:].rearrange("p (j q) -> p j q", q=P),
                op=ALU.subtract,
            )

        def store_distance(r, queue, over=None):
            y = sbuf("y%d" % r, [P, Q], F32, over)
            nc.scalar.activation(out=y[:].rearrange("p (j q) -> p j q", q=P), in_=diff[:, :, r, :], func=ACT.Abs)
            queue.dma_start(out=y_rows[r], in_=y[:])

        q_grouped = [
            regroup("q_grouped%d" % j, q_raw[:, :, block(j, P)], P, (vector_copy, scalar_copy)[j]) for j in range(Q_TILES)
        ]
        for j in range(Q_TILES):
            quantize(q_mx, q_grouped[j], block(j, P))
        a_banks = [score_keys(0, c) for c in range(T // BANK)]
        scalar_copy(a_sb[0][:, block(0, BANK)], a_banks[0][:])
        vector_copy(a_sb[0][:, block(1, BANK)], a_banks[1][:])
        q2_grouped = regroup("q2_grouped", q2_raw[:], Q, vector_copy)
        scalar_copy(a_sb[0][:, block(2, BANK)], a_banks[2][:])
        scalar_copy(a_sb[0][:, block(3, BANK)], a_banks[3][:])
        quantize(q2_mx, q2_grouped)
        for c in range(T // BANK):
            scalar_copy(a_sb[1][:, block(c, BANK)], score_keys(1, c)[:])

        pages_grouped0 = regroup("pages_grouped0", pages_raw[0][:], BANK, vector_copy)
        pages_mx0 = quantize_values("pages0", pages_grouped0, None)
        h_banks0 = [score_pages(j, pages_mx0) for j in range(Q_TILES)]
        a_picked0 = pick("a_picked0", a_sb[0], token_list[:], I, F32, scalar_copy)
        pages_grouped1 = regroup("pages_grouped1", pages_raw[1][:], BANK, vector_copy)
        pages_mx1 = quantize_values("pages1", pages_grouped1, None)
        for j in range(Q_TILES):
            scalar_copy(h_sb[j][:, block(0, BANK)], h_banks0[j][:])
        h_banks1 = [score_pages(j, pages_mx1) for j in range(Q_TILES)]
        a_picked1 = pick("a_picked1", a_sb[1], token_list[:], I, F32, vector_copy, over="pages_grouped1")
        for j in range(Q_TILES):
            scalar_copy(h_sb[j][:, block(1, BANK)], h_banks1[j][:])

        h_picked0 = pick("h_picked0", h_sb[0], page_list[:], I, F32, vector_copy)
        v_picked0 = pick("v_picked0", vals_sb[0], token_list[:], I, BF16, scalar_copy, over="pages1_codes")
        h_picked1 = pick("h_picked1", h_sb[1], page_list[:], I, F32, vector_copy)
        w_bank0 = turn_weights(0, a_picked0, h_picked0, over="h1")
        v_bank01 = value_bank([P, 2, 2, P])
        turn_values(v_picked0, v_bank01[:, 0])
        v_picked1 = pick("v_picked1", vals_sb[1], token_list[:], I, BF16, scalar_copy)
        w_bank1 = turn_weights(1, a_picked1, h_picked1)
        scale_weights(0, w_bank0)
        turn_values(v_picked1, v_bank01[:, 1])
        v_picked2 = pick("v_picked2", vals_sb[2], token_list[:], I, BF16, scalar_copy)
        scale_weights(1, w_bank1)
        quantize(w_mx, w_grouped)
        v_bank2 = value_bank([P, 1, 2, P])
        turn_values(v_picked2, v_bank2[:, 0])
        v_grouped01 = regroup_values("v_grouped01", v_bank01, over="vals2")
        v_picked3 = pick("v_picked3", vals_sb[3], token_list[:], I, BF16, vector_copy)
        v_mx01 = quantize_values("v01", v_grouped01, over="vals3")
        o_bank0 = mix_values(v_mx01, 0)
        o_bank1 = mix_values(v_mx01, 1)
        v_grouped2 = regroup_values("v_grouped2", v_bank2)
        m_picked0 = pick("m_picked0", member_sb[0], member_list[:], Q, F32, vector_copy)
        v_bank3 = value_bank([P, 1, 2, P])
        turn_values(v_picked3, v_bank3[:, 0])
        v_mx2 = quantize_values("v2", v_grouped2, over="member0")
        o_bank2 = mix_values(v_mx2, 0)
        subtract(0, o_bank0, m_picked0)
        m_picked1 = pick("m_picked1", member_sb[1], member_list[:], Q, F32, scalar_copy)
        v_grouped3 = regroup_values("v_grouped3", v_bank3, over="member1")
        subtract(1, o_bank1, m_picked1)
        m_picked2 = pick("m_picked2", member_sb[2], member_list[:], Q, F32, vector_copy)
        v_mx3 = quantize_values("v3", v_grouped3, over="member2")
        o_bank3 = mix_values(v_mx3, 0)
        store_distance(0, nc.sync, over="m_picked1")
        subtract(2, o_bank2, m_picked2)
        store_distance(1, nc.sync)

        m_picked3 = [
            pick(
                "m_picked3_%d" % j, member_sb[3], member_list[:, block(j, P // 16)], P, F32, (vector_copy, scalar_copy)[j]
            )
            for j in range(Q_TILES)
        ]
        store_distance(2, nc.sync, over="member3")
        for j in range(Q_TILES):
            subtract(3, o_bank3, m_picked3[j], block(j, 1))
        y_grouped = [sbuf("y_grouped%d" % j, [P, P, PACK], BF16) for j in range(Q_TILES)]
        grouped_lines, signed_lines = by_lines(y_grouped[0][:], diff[:, 0, :, :])
        nc.scalar.activation(out=grouped_lines, in_=signed_lines, func=ACT.Abs)
        signed = diff[:, 1, :, :].rearrange("p r q -> p q r")
        nc.vector.scalar_tensor_tensor(
            out=y_grouped[1][:], in0=signed, scalar=-1.0, in1=signed, op0=ALU.mult, op1=ALU.max
        )
        store_distance(3, nc.scalar)
        for j in range(Q_TILES):
            quantize(y_mx, y_grouped[j], block(j, P))
        y_codes, y_scales = y_mx
        nc.sync.dma_start(out=out_1[0].rearrange("p c r -> p (c r)").bitcast(I32), in_=y_codes[:].bitcast(I32))
        for row in range(4):
            queue = nc.scalar if row % 2 else nc.sync
            queue.dma_start(out=out_2[0, row:16:4, :].bitcast(I32), in_=y_scales[row:P:32, :].bitcast(I32))
